import numpy as np
import ml_dtypes


def mxq(x, axis, fmt="e4m3"):
    dtype, down = {"e4m3": (ml_dtypes.float8_e4m3fn, 7), "e5m2": (ml_dtypes.float8_e5m2, 14)}[fmt]
    v = np.moveaxis(np.asarray(x, np.float32).astype(ml_dtypes.bfloat16).astype(np.float64), axis, -1)
    blocks = v.reshape(v.shape[:-1] + (-1, 32))
    amax = np.abs(blocks).max(-1, keepdims=True)
    byte = np.maximum(np.where(amax > 0, np.frexp(amax)[1] - 1 + 127, 0) - down, 1)
    scale = np.exp2(byte - 127.0)
    codes = (blocks / scale).astype(np.float32).astype(dtype).astype(np.float64)
    return np.moveaxis((codes * scale).reshape(v.shape), -1, axis)


WIDE = False


def mx_kscale(k):
    if not WIDE:
        return np.ones(k)
    levels = np.array([10, -10, 5, -5, 0])
    if k % 512:
        return np.exp2(np.random.permutation(np.resize(levels, k // 32))).repeat(32)
    a = np.empty((k // 512, 16))
    for p in range(k // 512):
        a[p, :8] = np.random.permutation(np.resize(levels, 8))
        for g in range(8):
            far = levels[np.abs(levels - a[p, g]) >= 10]
            a[p, g + 8] = far[np.random.randint(len(far))]
    return np.exp2(a.ravel()).repeat(32)


def f64(x):
    return np.asarray(x).astype(np.float64)


def striped(idx):
    return np.tile(idx.reshape(-1, 16).T, (8, 1)).astype(np.uint16)


def unstriped(offs):
    return offs[:16].T.reshape(-1).astype(np.int64)


def silu(v):
    return v / (1.0 + np.exp(-np.maximum(v, -700.0)))


K, T, E, C, H, N = 512, 2048, 4, 256, 512, 256


def by_expert(wq, xq):
    return np.concatenate([wq[e].T @ xq[:, e * C:(e + 1) * C] for e in range(E)], axis=1)


def setup_inputs():
    n = np.random.standard_normal
    s = mx_kscale(K)[:, None]
    u = mx_kscale(H)
    return {
        "xT": (n((K, T)) * s).astype(np.float32),
        "w1": (n((E, K, H)) / np.sqrt(K) / s[None]).astype(np.float32),
        "w3": (n((E, K, H)) / np.sqrt(K) / s[None] * u[None, None, :]).astype(np.float32),
        "w2": (n((E, H, N)) / np.sqrt(H) / u[None, :, None]).astype(np.float32),
        "gate": np.tile(np.random.uniform(0.2, 1.0, E * C), (N, 1)).astype(np.float32),
        "offs": striped(np.random.permutation(T)[:E * C]),
        "dst": striped(np.random.permutation(T)[:E * C]),
    }


def reference(xT, w1, w3, w2, gate, offs, dst):
    idx = unstriped(offs)
    xq = mxq(f64(xT)[:, idx], 0, "e4m3")
    h = silu(by_expert(mxq(f64(w1), 1, "e4m3"), xq))
    h = h * by_expert(mxq(f64(w3), 1, "e4m3"), xq)
    y = by_expert(mxq(f64(w2), 1, "e4m3"), mxq(h, 0, "e4m3"))
    out = np.zeros((N, T))
    out[:, unstriped(dst)] = f64(gate) * y
    return out

@@ -1,0 +1,227 @@
+from contextlib import ExitStack
+
+import concourse.mybir as mybir
+
+K, T, E, C, H, N = 512, 2048, 4, 256, 512, 256
+FLOPS = 2 * E * C * (2 * K * H + H * N)
+
+F32 = mybir.dt.float32
+BF16 = mybir.dt.bfloat16
+U32 = mybir.dt.uint32
+I32 = mybir.dt.int32
+U16 = mybir.dt.uint16
+U8 = mybir.dt.uint8
+FP8X4 = mybir.dt.float8_e4m3fn_x4
+COPY = mybir.ActivationFunctionType.Copy
+SILU = mybir.ActivationFunctionType.Silu
+MULT = mybir.AluOpType.mult
+
+P = 128
+PACK = 4
+RUN = 4
+X_CHUNKS = (256, 512, 512, 512, 256)
+W1_VECTOR = (0, 128, 128, 64)
+W3_VECTOR = (128, 64, 64, 64)
+HALF = 128
+LIST_COLS = C // 16
+
+
+def split(nc, out, in_, at, total):
+    if at > 0:
+        nc.vector.tensor_copy(out=out(0, at), in_=in_(0, at))
+    if at < total:
+        nc.scalar.activation(out=out(at, total), in_=in_(at, total), func=COPY)
+
+
+def tile_moe_two_glu_silu_kernel(tc, xT, w1, w3, w2, gate, offs, dst, out):
+    nc = tc.nc
+    with ExitStack() as ctx:
+        keep = ctx.enter_context(tc.tile_pool(name="keep", bufs=1))
+        load = ctx.enter_context(tc.tile_pool(name="load", bufs=3))
+        cast = ctx.enter_context(tc.tile_pool(name="cast", bufs=2))
+        codes = ctx.enter_context(tc.tile_pool(name="codes", bufs=4))
+        hid = ctx.enter_context(tc.tile_pool(name="hid", bufs=3))
+        psum = ctx.enter_context(tc.psum_pool(name="psum", bufs=3))
+        psum_y = ctx.enter_context(tc.psum_pool(name="psum_y", bufs=2))
+
+        offs_sb = keep.tile([P, E * LIST_COLS], U16, name="offs_sb")
+        dst_sb = keep.tile([P, E * LIST_COLS], U16, name="dst_sb")
+        warm = keep.tile([P, 1], F32, name="warm")
+        windows = [keep.tile([P, T], F32, name=f"window{b}") for b in range(N // P)]
+        x_codes = keep.tile([P, T], U32, name="x_codes", align_bytes=64)
+        x_scales = keep.tile([P, T], U8, name="x_scales", align_bytes=64)
+        gates = [keep.tile([P, N // P, 2 * C], F32, name=f"gates{g}") for g in range(E // 2)]
+
+        def load_gate(g):
+            cols = slice(g * 2 * C, (g + 1) * 2 * C)
+            nc.sync.dma_start(out=gates[g][:], in_=gate[:, cols].rearrange("(b p) s -> p b s", p=P))
+
+        x_cols = [slice(sum(X_CHUNKS[:c]), sum(X_CHUNKS[:c + 1])) for c in range(len(X_CHUNKS))]
+        x_raw = []
+        for c, cols in enumerate(x_cols):
+            raw = keep.tile([P, PACK, X_CHUNKS[c]], F32, name=f"x_raw{c}")
+            nc.sync.dma_start(out=raw[:], in_=xT[:, cols].rearrange("(p j) t -> p j t", j=PACK))
+            x_raw.append(raw)
+            if c == 0:
+                nc.sync.dma_start(offs_sb[:], offs)
+
+        raws = []
+        for e in range(E):
+            tiles = {}
+            for name, w, width in (("w1", w1, H), ("w3", w3, H), ("w2", w2, N)):
+                if name == "w2" and e == E - 1:
+                    load_gate(E // 2 - 1)
+                tiles[name] = load.tile([P, PACK, width], F32, name=f"{name}_raw")
+                nc.sync.dma_start(out=tiles[name][:], in_=w[e].rearrange("(p j) n -> p j n", j=PACK))
+            raws.append(tiles)
+            if e == 0:
+                nc.sync.dma_start(dst_sb[:], dst)
+                load_gate(0)
+
+        nc.vector.memset(warm[:], 0.0)
+        nc.scalar.activation(out=warm[:], in_=warm[:], func=SILU)
+        nc.gpsimd.memset(x_scales[:].bitcast(I32), 0)
+        nc.vector.memset(windows[0][:], 0.0)
+        nc.gpsimd.memset(windows[1][:], 0.0)
+
+        for c, cols in enumerate(x_cols):
+            x_bf = cast.tile([P, X_CHUNKS[c] * PACK], BF16, name="x_bf", align_bytes=64)
+
+            def dst_view(a, b):
+                return x_bf[:, a * PACK:b * PACK].rearrange("p (c i j) -> p c j i", i=RUN, j=PACK)
+
+            def src_view(a, b):
+                return x_raw[c][:, :, a:b].rearrange("p j (c i) -> p c j i", i=RUN)
+
+            split(nc, dst_view, src_view, X_CHUNKS[c] * 5 // 8, X_CHUNKS[c])
+            nc.vector.quantize_mx(out=x_codes[:, cols].bitcast(FP8X4), scales=x_scales[:, cols], in_=x_bf[:])
+
+        def gather(e):
+            at = slice(e * LIST_COLS, (e + 1) * LIST_COLS)
+            words = codes.tile([P, C], U32, name="slot_codes", align_bytes=64)
+            planes = codes.tile([P, C], U8, name="slot_scales", align_bytes=64)
+            nc.vector.tensor_copy(out=words[:], in_=x_codes[:].indirect(offs_sb[:, at]))
+            nc.vector.tensor_copy(out=planes[:], in_=x_scales[:].indirect(offs_sb[:, at]))
+            return words, planes
+
+        def quantize_first(name, raw, at):
+            bf = cast.tile([P, PACK, H // PACK, PACK], BF16, name=f"{name}_bf", align_bytes=64)
+            out_codes = codes.tile([P, H], U32, name=f"{name}_codes", align_bytes=64)
+            out_scales = codes.tile([P, H], U8, name=f"{name}_scales", align_bytes=64)
+
+            def dst_view(a, b):
+                return bf[:, :, a // PACK:b // PACK, :].rearrange("p t m j -> p m j t")
+
+            def src_view(a, b):
+                return raw[:, :, a:b].rearrange("p j (m t) -> p m j t", t=PACK)
+
+            split(nc, dst_view, src_view, at, H)
+            nc.vector.quantize_mx(out=out_codes[:].bitcast(FP8X4), scales=out_scales[:], in_=bf[:].rearrange("p t m j -> p (t m j)"))
+            return out_codes, out_scales
+
+        def quantize_second(raw):
+            bf = cast.tile([P, N * PACK], BF16, name="w2_bf", align_bytes=64)
+            out_codes = codes.tile([P, N], U32, name="w2_codes", align_bytes=64)
+            out_scales = codes.tile([P, N], U8, name="w2_scales", align_bytes=64)
+
+            def dst_view(a, b):
+                return bf[:, a * PACK:b * PACK].rearrange("p (c i j) -> p c j i", i=RUN, j=PACK)
+
+            def src_view(a, b):
+                return raw[:, :, a:b].rearrange("p j (c i) -> p c j i", i=RUN)
+
+            split(nc, dst_view, src_view, 0, N)
+            nc.vector.quantize_mx(out=out_codes[:].bitcast(FP8X4), scales=out_scales[:], in_=bf[:])
+            return out_codes, out_scales
+
+        def first_product(bank_name, slots, weights):
+            banks = []
+            for s in range(C // HALF):
+                cols = slice(s * HALF, (s + 1) * HALF)
+                bank = psum.tile([P, PACK, HALF], F32, name=bank_name)
+                for t in range(PACK):
+                    w_cols = slice(t * P, (t + 1) * P)
+                    nc.tensor.matmul_mx(
+                        out=bank[:, t, :],
+                        lhsT=weights[0][:, w_cols].bitcast(FP8X4),
+                        lhsT_scale=weights[1][:, w_cols],
+                        rhs=slots[0][:, cols].bitcast(FP8X4),
+                        rhs_scale=slots[1][:, cols],
+                        start=True,
+                        stop=True,
+                    )
+                banks.append(bank)
+            return banks
+
+        def hidden(a_banks, b_banks):
+            h_bf = hid.tile([P, C, PACK], BF16, name="h_bf", align_bytes=64)
+            h_codes = hid.tile([P, C], U32, name="h_codes", align_bytes=64)
+            h_scales = hid.tile([P, C], U8, name="h_scales", align_bytes=64)
+            acts = []
+            for bank in a_banks:
+                act = hid.tile([P, HALF, PACK], F32, name="act")
+                nc.scalar.activation(out=act[:], in_=bank[:].rearrange("p t c -> p c t"), func=SILU)
+                acts.append(act)
+            for s, bank in enumerate(b_banks):
+                cols = slice(s * HALF, (s + 1) * HALF)
+                nc.vector.tensor_tensor(out=h_bf[:, cols, :], in0=acts[s][:], in1=bank[:].rearrange("p t c -> p c t"), op=MULT)
+            nc.vector.quantize_mx(out=h_codes[:].bitcast(FP8X4), scales=h_scales[:], in_=h_bf[:].rearrange("p c t -> p (c t)"))
+            return h_codes, h_scales
+
+        def project(h, second):
+            y_bank = psum_y.tile([P, N // P, C], F32, name="y_bank")
+            for b in range(N // P):
+                w_cols = slice(b * P, (b + 1) * P)
+                nc.tensor.matmul_mx(
+                    out=y_bank[:, b, :],
+                    lhsT=second[0][:, w_cols].bitcast(FP8X4),
+                    lhsT_scale=second[1][:, w_cols],
+                    rhs=h[0][:].bitcast(FP8X4),
+                    rhs_scale=h[1][:],
+                    start=True,
+                    stop=True,
+                )
+            return y_bank
+
+        def copy_out(y_bank, last):
+            y = hid.tile([P, N // P, C], F32, name="y")
+            if last:
+                for b in reversed(range(N // P)):
+                    nc.scalar.activation(out=y[:, b, :], in_=y_bank[:, b, :], func=COPY)
+            else:
+                nc.scalar.activation(out=y[:], in_=y_bank[:], func=COPY)
+            return y
+
+        def scatter(e, y, b):
+            at = slice(e * LIST_COLS, (e + 1) * LIST_COLS)
+            gate_cols = slice((e % 2) * C, (e % 2 + 1) * C)
+            nc.vector.tensor_tensor(
+                out=windows[b][:].indirect(dst_sb[:, at]),
+                in0=y[:, b, :],
+                in1=gates[e // 2][:, b, gate_cols],
+                op=MULT,
+            )
+
+        slots = [gather(e) for e in range(3)]
+        y_bank = None
+        y = None
+        for e in range(E):
+            first = quantize_first("w1", raws[e]["w1"], W1_VECTOR[e])
+            a_banks = first_product("a_bank", slots[e], first)
+            if e > 0:
+                y = copy_out(y_bank, False)
+                scatter(e - 1, y, 0)
+            third = quantize_first("w3", raws[e]["w3"], W3_VECTOR[e])
+            b_banks = first_product("b_bank", slots[e], third)
+            if 0 < e < E - 1:
+                scatter(e - 1, y, 1)
+            h = hidden(a_banks, b_banks)
+            second = quantize_second(raws[e]["w2"])
+            y_bank = project(h, second)
+            if e == 0:
+                slots.append(gather(3))
+        scatter(E - 2, y, 1)
+        y = copy_out(y_bank, True)
+        for b, queue in ((1, nc.scalar), (0, nc.sync)):
+            scatter(E - 1, y, b)
+            queue.dma_start(out=out[b * P:(b + 1) * P, :], in_=windows[b][:])

@@ -20,8 +20,8 @@ P = 128
 PACK = 4
 RUN = 4
 X_CHUNKS = (256, 512, 512, 512, 256)
-W1_VECTOR = (0, 128, 128, 64)
-W3_VECTOR = (128, 64, 64, 64)
+W1_VECTOR = (0, 0, 0, H)
+W3_VECTOR = (0, 0, 0, 0)
 HALF = 128
 LIST_COLS = C // 16
 
@@ -37,7 +37,7 @@ def tile_moe_two_glu_silu_kernel(tc, xT, w1, w3, w2, gate, offs, dst, out):
     nc = tc.nc
     with ExitStack() as ctx:
         keep = ctx.enter_context(tc.tile_pool(name="keep", bufs=1))
-        load = ctx.enter_context(tc.tile_pool(name="load", bufs=3))
+        load = ctx.enter_context(tc.tile_pool(name="load", bufs=2))
         cast = ctx.enter_context(tc.tile_pool(name="cast", bufs=2))
         codes = ctx.enter_context(tc.tile_pool(name="codes", bufs=4))
         hid = ctx.enter_context(tc.tile_pool(name="hid", bufs=3))
@@ -65,18 +65,19 @@ def tile_moe_two_glu_silu_kernel(tc, xT, w1, w3, w2, gate, offs, dst, out):
             if c == 0:
                 nc.sync.dma_start(offs_sb[:], offs)
 
-        raws = []
-        for e in range(E):
+        def load_weights(e):
             tiles = {}
             for name, w, width in (("w1", w1, H), ("w3", w3, H), ("w2", w2, N)):
                 if name == "w2" and e == E - 1:
                     load_gate(E // 2 - 1)
                 tiles[name] = load.tile([P, PACK, width], F32, name=f"{name}_raw")
                 nc.sync.dma_start(out=tiles[name][:], in_=w[e].rearrange("(p j) n -> p j n", j=PACK))
-            raws.append(tiles)
             if e == 0:
                 nc.sync.dma_start(dst_sb[:], dst)
                 load_gate(0)
+            return tiles
+
+        raws = [load_weights(0), load_weights(1)]
 
         nc.vector.memset(warm[:], 0.0)
         nc.scalar.activation(out=warm[:], in_=warm[:], func=SILU)
@@ -85,7 +86,7 @@ def tile_moe_two_glu_silu_kernel(tc, xT, w1, w3, w2, gate, offs, dst, out):
         nc.gpsimd.memset(windows[1][:], 0.0)
 
         for c, cols in enumerate(x_cols):
-            x_bf = cast.tile([P, X_CHUNKS[c] * PACK], BF16, name="x_bf", align_bytes=64)
+            x_bf = keep.tile([P, X_CHUNKS[c] * PACK], BF16, name=f"x_bf{c}", align_bytes=64)
 
             def dst_view(a, b):
                 return x_bf[:, a * PACK:b * PACK].rearrange("p (c i j) -> p c j i", i=RUN, j=PACK)
@@ -93,16 +94,17 @@ def tile_moe_two_glu_silu_kernel(tc, xT, w1, w3, w2, gate, offs, dst, out):
             def src_view(a, b):
                 return x_raw[c][:, :, a:b].rearrange("p j (c i) -> p c j i", i=RUN)
 
-            split(nc, dst_view, src_view, X_CHUNKS[c] * 5 // 8, X_CHUNKS[c])
+            split(nc, dst_view, src_view, X_CHUNKS[c] // 2, X_CHUNKS[c])
             nc.vector.quantize_mx(out=x_codes[:, cols].bitcast(FP8X4), scales=x_scales[:, cols], in_=x_bf[:])
 
-        def gather(e):
-            at = slice(e * LIST_COLS, (e + 1) * LIST_COLS)
-            words = codes.tile([P, C], U32, name="slot_codes", align_bytes=64)
-            planes = codes.tile([P, C], U8, name="slot_scales", align_bytes=64)
+        def gather(e0, e1):
+            at = slice(e0 * LIST_COLS, e1 * LIST_COLS)
+            words = keep.tile([P, (e1 - e0) * C], U32, name=f"slot_codes{e0}", align_bytes=64)
+            planes = keep.tile([P, (e1 - e0) * C], U8, name=f"slot_scales{e0}", align_bytes=64)
             nc.vector.tensor_copy(out=words[:], in_=x_codes[:].indirect(offs_sb[:, at]))
             nc.vector.tensor_copy(out=planes[:], in_=x_scales[:].indirect(offs_sb[:, at]))
-            return words, planes
+            for e in range(e0, e1):
+                slots[e] = (words, planes, (e - e0) * C)
 
         def quantize_first(name, raw, at):
             bf = cast.tile([P, PACK, H // PACK, PACK], BF16, name=f"{name}_bf", align_bytes=64)
@@ -119,25 +121,10 @@ def tile_moe_two_glu_silu_kernel(tc, xT, w1, w3, w2, gate, offs, dst, out):
             nc.vector.quantize_mx(out=out_codes[:].bitcast(FP8X4), scales=out_scales[:], in_=bf[:].rearrange("p t m j -> p (t m j)"))
             return out_codes, out_scales
 
-        def quantize_second(raw):
-            bf = cast.tile([P, N * PACK], BF16, name="w2_bf", align_bytes=64)
-            out_codes = codes.tile([P, N], U32, name="w2_codes", align_bytes=64)
-            out_scales = codes.tile([P, N], U8, name="w2_scales", align_bytes=64)
-
-            def dst_view(a, b):
-                return bf[:, a * PACK:b * PACK].rearrange("p (c i j) -> p c j i", i=RUN, j=PACK)
-
-            def src_view(a, b):
-                return raw[:, :, a:b].rearrange("p j (c i) -> p c j i", i=RUN)
-
-            split(nc, dst_view, src_view, 0, N)
-            nc.vector.quantize_mx(out=out_codes[:].bitcast(FP8X4), scales=out_scales[:], in_=bf[:])
-            return out_codes, out_scales
-
         def first_product(bank_name, slots, weights):
             banks = []
             for s in range(C // HALF):
-                cols = slice(s * HALF, (s + 1) * HALF)
+                cols = slice(slots[2] + s * HALF, slots[2] + (s + 1) * HALF)
                 bank = psum.tile([P, PACK, HALF], F32, name=bank_name)
                 for t in range(PACK):
                     w_cols = slice(t * P, (t + 1) * P)
@@ -153,22 +140,30 @@ def tile_moe_two_glu_silu_kernel(tc, xT, w1, w3, w2, gate, offs, dst, out):
                 banks.append(bank)
             return banks
 
-        def hidden(a_banks, b_banks):
-            h_bf = hid.tile([P, C, PACK], BF16, name="h_bf", align_bytes=64)
-            h_codes = hid.tile([P, C], U32, name="h_codes", align_bytes=64)
-            h_scales = hid.tile([P, C], U8, name="h_scales", align_bytes=64)
+        def activate(a_banks):
             acts = []
             for bank in a_banks:
-                act = hid.tile([P, HALF, PACK], F32, name="act")
+                act = hid.tile([P, HALF, PACK], F32, name="act", bufs=4)
                 nc.scalar.activation(out=act[:], in_=bank[:].rearrange("p t c -> p c t"), func=SILU)
                 acts.append(act)
-            for s, bank in enumerate(b_banks):
-                cols = slice(s * HALF, (s + 1) * HALF)
-                nc.vector.tensor_tensor(out=h_bf[:, cols, :], in0=acts[s][:], in1=bank[:].rearrange("p t c -> p c t"), op=MULT)
-            nc.vector.quantize_mx(out=h_codes[:].bitcast(FP8X4), scales=h_scales[:], in_=h_bf[:].rearrange("p c t -> p (c t)"))
-            return h_codes, h_scales
+            return acts
 
-        def project(h, second):
+        def second_operands(acts, b_banks, w2_raw):
+            bf = hid.tile([P, N + C, PACK], BF16, name="second_bf", align_bytes=64)
+            out_codes = hid.tile([P, N + C], U32, name="second_codes", align_bytes=64)
+            out_scales = hid.tile([P, N + C], U8, name="second_scales", align_bytes=64)
+            nc.scalar.activation(
+                out=bf[:, :N, :].rearrange("p (c i) j -> p c j i", i=RUN),
+                in_=w2_raw[:].rearrange("p j (c i) -> p c j i", i=RUN),
+                func=COPY,
+            )
+            for s, bank in enumerate(b_banks):
+                cols = slice(N + s * HALF, N + (s + 1) * HALF)
+                nc.vector.tensor_tensor(out=bf[:, cols, :], in0=acts[s][:], in1=bank[:].rearrange("p t c -> p c t"), op=MULT)
+            nc.vector.quantize_mx(out=out_codes[:].bitcast(FP8X4), scales=out_scales[:], in_=bf[:].rearrange("p c t -> p (c t)"))
+            return out_codes, out_scales
+
+        def project(second):
             y_bank = psum_y.tile([P, N // P, C], F32, name="y_bank")
             for b in range(N // P):
                 w_cols = slice(b * P, (b + 1) * P)
@@ -176,8 +171,8 @@ def tile_moe_two_glu_silu_kernel(tc, xT, w1, w3, w2, gate, offs, dst, out):
                     out=y_bank[:, b, :],
                     lhsT=second[0][:, w_cols].bitcast(FP8X4),
                     lhsT_scale=second[1][:, w_cols],
-                    rhs=h[0][:].bitcast(FP8X4),
-                    rhs_scale=h[1][:],
+                    rhs=second[0][:, N:].bitcast(FP8X4),
+                    rhs_scale=second[1][:, N:],
                     start=True,
                     stop=True,
                 )
@@ -202,25 +197,29 @@ def tile_moe_two_glu_silu_kernel(tc, xT, w1, w3, w2, gate, offs, dst, out):
                 op=MULT,
             )
 
-        slots = [gather(e) for e in range(3)]
-        y_bank = None
-        y = None
+        slots = {}
+        gather(0, 1)
         for e in range(E):
             first = quantize_first("w1", raws[e]["w1"], W1_VECTOR[e])
             a_banks = first_product("a_bank", slots[e], first)
-            if e > 0:
+            if e == 0:
+                gather(1, 2)
+            else:
                 y = copy_out(y_bank, False)
-                scatter(e - 1, y, 0)
             third = quantize_first("w3", raws[e]["w3"], W3_VECTOR[e])
             b_banks = first_product("b_bank", slots[e], third)
-            if 0 < e < E - 1:
-                scatter(e - 1, y, 1)
-            h = hidden(a_banks, b_banks)
-            second = quantize_second(raws[e]["w2"])
-            y_bank = project(h, second)
+            acts = activate(a_banks)
             if e == 0:
-                slots.append(gather(3))
-        scatter(E - 2, y, 1)
+                gather(2, 3)
+            else:
+                scatter(e - 1, y, 0)
+            y_bank = project(second_operands(acts, b_banks, raws[e]["w2"]))
+            if e == 0:
+                gather(3, 4)
+            else:
+                scatter(e - 1, y, 1)
+            if e + 2 < E:
+                raws.append(load_weights(e + 2))
         y = copy_out(y_bank, True)
         for b, queue in ((1, nc.scalar), (0, nc.sync)):
             scatter(E - 1, y, b)

from contextlib import ExitStack

import concourse.mybir as mybir

K, T, E, C, H, N = 512, 2048, 4, 256, 512, 256
FLOPS = 2 * E * C * (2 * K * H + H * N)

F32 = mybir.dt.float32
BF16 = mybir.dt.bfloat16
U32 = mybir.dt.uint32
I32 = mybir.dt.int32
U16 = mybir.dt.uint16
U8 = mybir.dt.uint8
FP8X4 = mybir.dt.float8_e4m3fn_x4
COPY = mybir.ActivationFunctionType.Copy
SILU = mybir.ActivationFunctionType.Silu
MULT = mybir.AluOpType.mult

P = 128
PACK = 4
RUN = 4
X_CHUNKS = (256, 512, 512, 512, 256)
W1_VECTOR = (0, 0, 0, H)
W3_VECTOR = (0, 0, 0, 0)
HALF = 128
LIST_COLS = C // 16


def split(nc, out, in_, at, total):
    if at > 0:
        nc.vector.tensor_copy(out=out(0, at), in_=in_(0, at))
    if at < total:
        nc.scalar.activation(out=out(at, total), in_=in_(at, total), func=COPY)


def tile_moe_two_glu_silu_kernel(tc, xT, w1, w3, w2, gate, offs, dst, out):
    nc = tc.nc
    with ExitStack() as ctx:
        keep = ctx.enter_context(tc.tile_pool(name="keep", bufs=1))
        load = ctx.enter_context(tc.tile_pool(name="load", bufs=2))
        cast = ctx.enter_context(tc.tile_pool(name="cast", bufs=2))
        codes = ctx.enter_context(tc.tile_pool(name="codes", bufs=4))
        hid = ctx.enter_context(tc.tile_pool(name="hid", bufs=3))
        psum = ctx.enter_context(tc.psum_pool(name="psum", bufs=3))
        psum_y = ctx.enter_context(tc.psum_pool(name="psum_y", bufs=2))

        offs_sb = keep.tile([P, E * LIST_COLS], U16, name="offs_sb")
        dst_sb = keep.tile([P, E * LIST_COLS], U16, name="dst_sb")
        warm = keep.tile([P, 1], F32, name="warm")
        windows = [keep.tile([P, T], F32, name=f"window{b}") for b in range(N // P)]
        x_codes = keep.tile([P, T], U32, name="x_codes", align_bytes=64)
        x_scales = keep.tile([P, T], U8, name="x_scales", align_bytes=64)
        gates = [keep.tile([P, N // P, 2 * C], F32, name=f"gates{g}") for g in range(E // 2)]

        def load_gate(g):
            cols = slice(g * 2 * C, (g + 1) * 2 * C)
            nc.sync.dma_start(out=gates[g][:], in_=gate[:, cols].rearrange("(b p) s -> p b s", p=P))

        x_cols = [slice(sum(X_CHUNKS[:c]), sum(X_CHUNKS[:c + 1])) for c in range(len(X_CHUNKS))]
        x_raw = []
        for c, cols in enumerate(x_cols):
            raw = keep.tile([P, PACK, X_CHUNKS[c]], F32, name=f"x_raw{c}")
            nc.sync.dma_start(out=raw[:], in_=xT[:, cols].rearrange("(p j) t -> p j t", j=PACK))
            x_raw.append(raw)
            if c == 0:
                nc.sync.dma_start(offs_sb[:], offs)

        def load_weights(e):
            tiles = {}
            for name, w, width in (("w1", w1, H), ("w3", w3, H), ("w2", w2, N)):
                if name == "w2" and e == E - 1:
                    load_gate(E // 2 - 1)
                tiles[name] = load.tile([P, PACK, width], F32, name=f"{name}_raw")
                nc.sync.dma_start(out=tiles[name][:], in_=w[e].rearrange("(p j) n -> p j n", j=PACK))
            if e == 0:
                nc.sync.dma_start(dst_sb[:], dst)
                load_gate(0)
            return tiles

        raws = [load_weights(0), load_weights(1)]

        nc.vector.memset(warm[:], 0.0)
        nc.scalar.activation(out=warm[:], in_=warm[:], func=SILU)
        nc.gpsimd.memset(x_scales[:].bitcast(I32), 0)
        nc.vector.memset(windows[0][:], 0.0)
        nc.gpsimd.memset(windows[1][:], 0.0)

        for c, cols in enumerate(x_cols):
            x_bf = keep.tile([P, X_CHUNKS[c] * PACK], BF16, name=f"x_bf{c}", align_bytes=64)

            def dst_view(a, b):
                return x_bf[:, a * PACK:b * PACK].rearrange("p (c i j) -> p c j i", i=RUN, j=PACK)

            def src_view(a, b):
                return x_raw[c][:, :, a:b].rearrange("p j (c i) -> p c j i", i=RUN)

            split(nc, dst_view, src_view, X_CHUNKS[c] // 2, X_CHUNKS[c])
            nc.vector.quantize_mx(out=x_codes[:, cols].bitcast(FP8X4), scales=x_scales[:, cols], in_=x_bf[:])

        def gather(e0, e1):
            at = slice(e0 * LIST_COLS, e1 * LIST_COLS)
            words = keep.tile([P, (e1 - e0) * C], U32, name=f"slot_codes{e0}", align_bytes=64)
            planes = keep.tile([P, (e1 - e0) * C], U8, name=f"slot_scales{e0}", align_bytes=64)
            nc.vector.tensor_copy(out=words[:], in_=x_codes[:].indirect(offs_sb[:, at]))
            nc.vector.tensor_copy(out=planes[:], in_=x_scales[:].indirect(offs_sb[:, at]))
            for e in range(e0, e1):
                slots[e] = (words, planes, (e - e0) * C)

        def quantize_first(name, raw, at):
            bf = cast.tile([P, PACK, H // PACK, PACK], BF16, name=f"{name}_bf", align_bytes=64)
            out_codes = codes.tile([P, H], U32, name=f"{name}_codes", align_bytes=64)
            out_scales = codes.tile([P, H], U8, name=f"{name}_scales", align_bytes=64)

            def dst_view(a, b):
                return bf[:, :, a // PACK:b // PACK, :].rearrange("p t m j -> p m j t")

            def src_view(a, b):
                return raw[:, :, a:b].rearrange("p j (m t) -> p m j t", t=PACK)

            split(nc, dst_view, src_view, at, H)
            nc.vector.quantize_mx(out=out_codes[:].bitcast(FP8X4), scales=out_scales[:], in_=bf[:].rearrange("p t m j -> p (t m j)"))
            return out_codes, out_scales

        def first_product(bank_name, slots, weights):
            banks = []
            for s in range(C // HALF):
                cols = slice(slots[2] + s * HALF, slots[2] + (s + 1) * HALF)
                bank = psum.tile([P, PACK, HALF], F32, name=bank_name)
                for t in range(PACK):
                    w_cols = slice(t * P, (t + 1) * P)
                    nc.tensor.matmul_mx(
                        out=bank[:, t, :],
                        lhsT=weights[0][:, w_cols].bitcast(FP8X4),
                        lhsT_scale=weights[1][:, w_cols],
                        rhs=slots[0][:, cols].bitcast(FP8X4),
                        rhs_scale=slots[1][:, cols],
                        start=True,
                        stop=True,
                    )
                banks.append(bank)
            return banks

        def activate(a_banks):
            acts = []
            for bank in a_banks:
                act = hid.tile([P, HALF, PACK], F32, name="act", bufs=4)
                nc.scalar.activation(out=act[:], in_=bank[:].rearrange("p t c -> p c t"), func=SILU)
                acts.append(act)
            return acts

        def second_operands(acts, b_banks, w2_raw):
            bf = hid.tile([P, N + C, PACK], BF16, name="second_bf", align_bytes=64)
            out_codes = hid.tile([P, N + C], U32, name="second_codes", align_bytes=64)
            out_scales = hid.tile([P, N + C], U8, name="second_scales", align_bytes=64)
            nc.scalar.activation(
                out=bf[:, :N, :].rearrange("p (c i) j -> p c j i", i=RUN),
                in_=w2_raw[:].rearrange("p j (c i) -> p c j i", i=RUN),
                func=COPY,
            )
            for s, bank in enumerate(b_banks):
                cols = slice(N + s * HALF, N + (s + 1) * HALF)
                nc.vector.tensor_tensor(out=bf[:, cols, :], in0=acts[s][:], in1=bank[:].rearrange("p t c -> p c t"), op=MULT)
            nc.vector.quantize_mx(out=out_codes[:].bitcast(FP8X4), scales=out_scales[:], in_=bf[:].rearrange("p c t -> p (c t)"))
            return out_codes, out_scales

        def project(second):
            y_bank = psum_y.tile([P, N // P, C], F32, name="y_bank")
            for b in range(N // P):
                w_cols = slice(b * P, (b + 1) * P)
                nc.tensor.matmul_mx(
                    out=y_bank[:, b, :],
                    lhsT=second[0][:, w_cols].bitcast(FP8X4),
                    lhsT_scale=second[1][:, w_cols],
                    rhs=second[0][:, N:].bitcast(FP8X4),
                    rhs_scale=second[1][:, N:],
                    start=True,
                    stop=True,
                )
            return y_bank

        def copy_out(y_bank, last):
            y = hid.tile([P, N // P, C], F32, name="y")
            if last:
                for b in reversed(range(N // P)):
                    nc.scalar.activation(out=y[:, b, :], in_=y_bank[:, b, :], func=COPY)
            else:
                nc.scalar.activation(out=y[:], in_=y_bank[:], func=COPY)
            return y

        def scatter(e, y, b):
            at = slice(e * LIST_COLS, (e + 1) * LIST_COLS)
            gate_cols = slice((e % 2) * C, (e % 2 + 1) * C)
            nc.vector.tensor_tensor(
                out=windows[b][:].indirect(dst_sb[:, at]),
                in0=y[:, b, :],
                in1=gates[e // 2][:, b, gate_cols],
                op=MULT,
            )

        slots = {}
        gather(0, 1)
        for e in range(E):
            first = quantize_first("w1", raws[e]["w1"], W1_VECTOR[e])
            a_banks = first_product("a_bank", slots[e], first)
            if e == 0:
                gather(1, 2)
            else:
                y = copy_out(y_bank, False)
            third = quantize_first("w3", raws[e]["w3"], W3_VECTOR[e])
            b_banks = first_product("b_bank", slots[e], third)
            acts = activate(a_banks)
            if e == 0:
                gather(2, 3)
            else:
                scatter(e - 1, y, 0)
            y_bank = project(second_operands(acts, b_banks, raws[e]["w2"]))
            if e == 0:
                gather(3, 4)
            else:
                scatter(e - 1, y, 1)
            if e + 2 < E:
                raws.append(load_weights(e + 2))
        y = copy_out(y_bank, True)
        for b, queue in ((1, nc.scalar), (0, nc.sync)):
            scatter(E - 1, y, b)
            queue.dma_start(out=out[b * P:(b + 1) * P, :], in_=windows[b][:])
